import numpy as np
import ml_dtypes


def mxq(x, axis, fmt="e4m3"):
    dtype, down = {"e4m3": (ml_dtypes.float8_e4m3fn, 7), "e5m2": (ml_dtypes.float8_e5m2, 14)}[fmt]
    v = np.moveaxis(np.asarray(x, np.float32).astype(ml_dtypes.bfloat16).astype(np.float64), axis, -1)
    blocks = v.reshape(v.shape[:-1] + (-1, 32))
    amax = np.abs(blocks).max(-1, keepdims=True)
    byte = np.maximum(np.where(amax > 0, np.frexp(amax)[1] - 1 + 127, 0) - down, 1)
    scale = np.exp2(byte - 127.0)
    codes = (blocks / scale).astype(np.float32).astype(dtype).astype(np.float64)
    return np.moveaxis((codes * scale).reshape(v.shape), -1, axis)


WIDE = False


def mx_kscale(k):
    if not WIDE:
        return np.ones(k)
    levels = np.array([10, -10, 5, -5, 0])
    if k % 512:
        return np.exp2(np.random.permutation(np.resize(levels, k // 32))).repeat(32)
    a = np.empty((k // 512, 16))
    for p in range(k // 512):
        a[p, :8] = np.random.permutation(np.resize(levels, 8))
        for g in range(8):
            far = levels[np.abs(levels - a[p, g]) >= 10]
            a[p, g + 8] = far[np.random.randint(len(far))]
    return np.exp2(a.ravel()).repeat(32)


def f64(x):
    return np.asarray(x).astype(np.float64)


def striped(idx):
    return np.tile(idx.reshape(-1, 16).T, (8, 1)).astype(np.uint16)


def unstriped(offs):
    return offs[:16].T.reshape(-1).astype(np.int64)


def striped8(idx):
    return np.concatenate([x.reshape(-1, 16).T for x in idx]).astype(np.uint16)


def runs(offs, k):
    lists = np.stack([offs[16 * r : 16 * r + 16].T.reshape(-1) for r in range(8)]).astype(np.int64)
    return lists[np.arange(k) % 512 // 64]


def pack_weight(w):
    k, n = w.shape
    w = f64(np.asarray(w, np.float32).astype(ml_dtypes.bfloat16)).reshape(k // 32, 32, n)
    amax = np.abs(w).max(1)
    byte = np.clip(np.where(amax > 0, np.frexp(amax)[1] - 1 + 127 - 7, 1), 1, 254)
    scaled = (w * np.exp2(127.0 - byte)[:, None, :]).reshape(k, n).astype(np.float32)
    words = np.ascontiguousarray(scaled.reshape(k // 512, 128, 4, n).transpose(0, 1, 3, 2)).astype(ml_dtypes.float8_e4m3fn).view(np.uint8)
    return words, np.ascontiguousarray(byte.astype(np.uint8).reshape(k // 512, 16, n))


def unpack_weight(words, scales):
    g, p, n, _ = words.shape
    vals = np.ascontiguousarray(words).view(ml_dtypes.float8_e4m3fn).astype(np.float64) * np.repeat(np.exp2(scales.astype(np.float64) - 127.0), 8, axis=1)[..., None]
    return vals.transpose(0, 1, 3, 2).reshape(g * 512, n)


E2M1 = np.array([0.0, 0.5, 1.0, 1.5, 2.0, 3.0, 4.0, 6.0, -0.0, -0.5, -1.0, -1.5, -2.0, -3.0, -4.0, -6.0])


def pack_fp4(w):
    k, n = w.shape
    w = f64(np.asarray(w, np.float32).astype(ml_dtypes.bfloat16)).reshape(k // 32, 32, n)
    amax = np.abs(w).max(1)
    mant, ex = np.frexp(amax / 6.0)
    byte = np.clip(np.where(amax > 0, np.where(mant > 0.5, ex, ex - 1) + 127, 1), 1, 254)
    scaled = (w * np.exp2(127.0 - byte)[:, None, :]).reshape(k, n).astype(np.float32)
    c = np.ascontiguousarray(scaled.reshape(k // 512, 128, 4, n).transpose(0, 1, 3, 2)).astype(ml_dtypes.float4_e2m1fn).view(np.uint8) & 0xF
    words = (c[..., 0::2] | (c[..., 1::2] << 4)).reshape(k // 512, 128, 2 * n)
    return np.ascontiguousarray(words), np.ascontiguousarray(byte.astype(np.uint8).reshape(k // 512, 16, n))


def unpack_fp4(words, scales):
    g, _, n = scales.shape
    words = np.ascontiguousarray(words).reshape(g, 128, n, 2)
    nib = np.empty((g, 128, n, 4), np.uint8)
    nib[..., 0::2] = words & 0xF
    nib[..., 1::2] = words >> 4
    vals = E2M1[nib] * np.repeat(np.exp2(scales.astype(np.float64) - 127.0), 8, axis=1)[..., None]
    return vals.transpose(0, 1, 3, 2).reshape(g * 512, n)


def planes(y):
    n, m = y.shape
    v = y.astype(np.float32).astype(ml_dtypes.bfloat16).astype(np.float64).reshape(n // 32, 32, m)
    top = np.abs(v).max(1)
    byte = np.clip(np.where(top > 0, np.frexp(top)[1] - 1 + 127 - 7, 1), 1, 254)
    codes = (v * np.exp2(127.0 - byte)[:, None, :]).reshape(n, m).astype(np.float32).astype(ml_dtypes.float8_e4m3fn).view(np.uint8)
    words = codes.reshape(n // 512, 128, 4, m).transpose(0, 1, 3, 2)
    return np.ascontiguousarray(words), np.ascontiguousarray(byte.astype(np.uint8).reshape(n // 512, 16, m))


K, T, S, H, C = 512, 2048, 512, 512, 512


def setup_inputs():
    n = np.random.standard_normal
    s = mx_kscale(K)[:, None]
    packed_xT = pack_weight(n((K, T)) * s)
    packed_w1 = pack_fp4(n((K, H)) / np.sqrt(K) / s)
    packed_w2 = pack_fp4(n((K, H)) / np.sqrt(K) / s)
    return {
        "x_words": packed_xT[0],
        "x_scales": packed_xT[1],
        "w1_words": packed_w1[0],
        "w1_scales": packed_w1[1],
        "w2_words": packed_w2[0],
        "w2_scales": packed_w2[1],
        "gs": (np.random.uniform(0.5, 1.5, (K, 1)) / s).astype(np.float32),
        "offs": striped(np.random.permutation(T)[:S]),
        "two": striped(np.random.permutation(T)[:S]),
        "la": striped8(np.stack([np.random.permutation(S) for _ in range(8)])),
        "lb": striped8(np.stack([np.random.permutation(S) for _ in range(8)])),
        "cand": striped(np.random.permutation(T)[:C]),
    }


def reference(x_words, x_scales, w1_words, w1_scales, w2_words, w2_scales, gs, offs, two, la, lb, cand):
    x_cand = unpack_weight(x_words, x_scales)[:, unstriped(cand)]
    x_two = unpack_weight(x_words, x_scales)[:, unstriped(two)]
    c = unpack_fp4(w2_words, w2_scales).T @ x_two
    pr = np.exp(0.5 * c)
    pa = pr[np.arange(H)[:, None], runs(la, H)]
    xq = unpack_weight(x_words, x_scales)[:, unstriped(offs)]
    y = unpack_fp4(w1_words, w1_scales).T @ xq
    pb = pr[np.arange(H)[:, None], runs(lb, H)]
    z = f64(gs) * ((pa * (y[np.arange(H)[:, None], runs(la, H)]) + pb * (y[np.arange(H)[:, None], runs(lb, H)])) / (pa + pb + 1))
    out_0 = 0.0625 * ((x_cand.T @ mxq(z, 0, "e4m3")))
    return (out_0,) + planes(out_0)

@@ -1,0 +1,209 @@
+from contextlib import ExitStack
+
+import concourse.mybir as mybir
+
+K, T, S, H, C = 512, 2048, 512, 512, 512
+FLOPS = 2 * K * H * S * 2 + 2 * K * C * S
+
+F32 = mybir.dt.float32
+BF16 = mybir.dt.bfloat16
+I32 = mybir.dt.int32
+U32 = mybir.dt.uint32
+U16 = mybir.dt.uint16
+U8 = mybir.dt.uint8
+FP8X4 = mybir.dt.float8_e4m3fn_x4
+FP4X4 = mybir.dt.float4_e2m1fn_x4
+ACT = mybir.ActivationFunctionType
+ALU = mybir.AluOpType
+
+P = 128
+PACK = 4
+QUADS = 4
+LANES = 16
+BANK_COLS = 128
+PIECES = ((0, 256), (256, 128), (384, 128))
+
+
+def load_scale_rows(queue, plane, rows):
+    for q in range(QUADS):
+        queue.dma_start(out=plane[32 * q : 32 * q + 4, :].bitcast(I32), in_=rows[4 * q : 4 * q + 4, :].bitcast(I32))
+
+
+def dealt(ap):
+    return ap.rearrange("p (t m) -> p t m", t=PACK)
+
+
+def undealt(ap):
+    return ap.rearrange("p (m t) -> p t m", t=PACK)
+
+
+def tile_picked_gaussprod_none_po_kernel(
+    tc, x_words, x_scales, w1_words, w1_scales, w2_words, w2_scales, gs, offs, two, la, lb, cand, out_0, out_1, out_2
+):
+    nc = tc.nc
+    with ExitStack() as ctx:
+        lists = ctx.enter_context(tc.tile_pool(name="lists", bufs=1))
+        keep = ctx.enter_context(tc.tile_pool(name="keep", bufs=1))
+        psum = ctx.enter_context(tc.psum_pool(name="psum", bufs=8))
+
+        two_l = lists.tile([P, S // LANES], U16, name="two_l")
+        offs_l = lists.tile([P, S // LANES], U16, name="offs_l")
+        cand_l = lists.tile([P, C // LANES], U16, name="cand_l")
+        la_l = lists.tile([P, S // LANES], U16, name="la_l")
+        lb_l = lists.tile([P, S // LANES], U16, name="lb_l")
+
+        xw = keep.tile([P, T], U32, name="xw", align_bytes=64)
+        xs = keep.tile([P, T], U8, name="xs", align_bytes=64)
+        w1w = keep.tile([P, 2 * H], U8, name="w1w", align_bytes=64)
+        w2w = keep.tile([P, 2 * H], U8, name="w2w", align_bytes=64)
+        w1s = keep.tile([P, H], U8, name="w1s", align_bytes=64)
+        w2s = keep.tile([P, H], U8, name="w2s", align_bytes=64)
+        gain = keep.tile([P, PACK], F32, name="gain")
+
+        nc.gpsimd.memset(xs[:].bitcast(I32), 0)
+        nc.vector.memset(w2s[:].bitcast(I32), 0)
+        nc.vector.memset(w1s[:].bitcast(I32), 0)
+
+        nc.sync.dma_start(two_l[:], two)
+        nc.sync.dma_start(offs_l[:], offs)
+        nc.sync.dma_start(out=w2w[:].bitcast(I32), in_=w2_words[0].bitcast(I32))
+        load_scale_rows(nc.sync, xs, x_scales[0])
+        nc.sync.dma_start(out=xw[:].bitcast(I32), in_=x_words[0].rearrange("p c r -> p (c r)").bitcast(I32))
+        load_scale_rows(nc.scalar, w2s, w2_scales[0])
+        nc.sync.dma_start(out=w1w[:].bitcast(I32), in_=w1_words[0].bitcast(I32))
+        nc.sync.dma_start(la_l[:], la)
+        nc.sync.dma_start(cand_l[:], cand)
+        load_scale_rows(nc.sync, w1s, w1_scales[0])
+        nc.sync.dma_start(lb_l[:], lb)
+        nc.gpsimd.dma_start(out=gain[:], in_=gs.rearrange("(p t) o -> p (t o)", t=PACK))
+
+        def picked(name, offsets):
+            words = keep.tile([P, S], U32, name=name + "_w", align_bytes=64)
+            scales = keep.tile([P, S], U8, name=name + "_s", align_bytes=64)
+            return words, scales, offsets
+
+        def gather_scales(pick):
+            nc.vector.tensor_copy(pick[1][:], xs[:].indirect(pick[2][:]))
+
+        def gather_words(pick):
+            nc.vector.tensor_copy(pick[0][:], xw[:].indirect(pick[2][:]))
+
+        def deal_weight(name, words, scales):
+            words_d = keep.tile([P, 2 * H], U8, name=name + "_wd", align_bytes=64)
+            scales_d = keep.tile([P, H], U8, name=name + "_sd", align_bytes=64)
+            nc.scalar.copy(dealt(words_d[:].bitcast(U16)), undealt(words[:].bitcast(U16)))
+            nc.vector.tensor_copy(dealt(scales_d[:]), undealt(scales[:]))
+            return words_d, scales_d
+
+        x_two, x_idx, x_cand = picked("two", two_l), picked("idx", offs_l), picked("cand", cand_l)
+        gather_scales(x_two)
+        gather_scales(x_idx)
+        w2 = deal_weight("w2", w2w, w2s)
+        gather_words(x_two)
+        w1 = deal_weight("w1", w1w, w1s)
+        gather_words(x_idx)
+
+        def project(weight, pick, t):
+            bank = psum.tile([P, S], F32, name="bank")
+            nc.tensor.matmul_mx(
+                out=bank[:],
+                lhsT=weight[0][:, 2 * P * t : 2 * P * (t + 1)].bitcast(FP4X4),
+                lhsT_scale=weight[1][:, P * t : P * (t + 1)],
+                rhs=pick[0][:].bitcast(FP8X4),
+                rhs_scale=pick[1][:],
+                start=True,
+                stop=True,
+            )
+            return bank
+
+        pr, u = [], []
+        for t in range(PACK):
+            c_t = project(w2, x_two, t)
+            pr_t = keep.tile([P, S], F32, name="pr%d" % t)
+            nc.scalar.activation(pr_t[:], c_t[:], ACT.Exp, scale=0.5)
+            pr.append(pr_t)
+        for t in range(PACK):
+            y_t = project(w1, x_idx, t)
+            u_t = keep.tile([P, S], F32, name="u%d" % t)
+            nc.vector.scalar_tensor_tensor(u_t[:], y_t[:], gain[:, t : t + 1], pr[t][:], ALU.mult, ALU.mult)
+            u.append(u_t)
+
+        gather_scales(x_cand)
+        gather_words(x_cand)
+        cand_w = keep.tile([P, C], U32, name="cand_wd", align_bytes=64)
+        cand_s = keep.tile([P, C], U8, name="cand_sd", align_bytes=64)
+        nc.vector.tensor_copy(dealt(cand_w[:]), undealt(x_cand[0][:]))
+        nc.vector.tensor_copy(dealt(cand_s[:]), undealt(x_cand[1][:]))
+
+        out_w = keep.tile([P, S], U32, name="out_w", align_bytes=64)
+        out_s = keep.tile([P, S], U8, name="out_s", align_bytes=64)
+        out_rows = out_0.rearrange("(p t) j -> p t j", t=PACK)
+        out_words = out_1[0].rearrange("p c r -> p (c r)").bitcast(I32)
+
+        def fetch_sum(name, tables, j0, n):
+            first = keep.tile([P, PACK, n], F32, name=name + "_a%d" % j0)
+            total = keep.tile([P, PACK, n], F32, name=name + "_ab%d" % j0)
+            cols = slice(j0 // LANES, (j0 + n) // LANES)
+            for t in range(PACK):
+                nc.scalar.activation(first[:, t, :], tables[t][:].indirect(la_l[:, cols]), ACT.Copy)
+                nc.vector.tensor_tensor(total[:, t, :], tables[t][:].indirect(lb_l[:, cols]), first[:, t, :], ALU.add)
+            return total
+
+        def make_z(j0, n):
+            den = fetch_sum("p", pr, j0, n)
+            num = fetch_sum("u", u, j0, n)
+            root = keep.tile([P, PACK, n], F32, name="root%d" % j0)
+            inv = keep.tile([P, PACK, n], F32, name="inv%d" % j0)
+            nc.scalar.activation(root[:], den[:], ACT.Abs_reciprocal_sqrt, bias=1.0)
+            nc.scalar.activation(inv[:], root[:], ACT.Square)
+            z16 = keep.tile([P, n, PACK], BF16, name="z16_%d" % j0, align_bytes=64)
+            nc.vector.tensor_tensor(
+                z16[:].rearrange("p (c i) t -> p c t i", i=4),
+                num[:].rearrange("p t (c i) -> p c t i", i=4),
+                inv[:].rearrange("p t (c i) -> p c t i", i=4),
+                ALU.mult,
+            )
+            z_w = keep.tile([P, n], U32, name="z_w%d" % j0, align_bytes=64)
+            z_s = keep.tile([P, n], U8, name="z_s%d" % j0, align_bytes=64)
+            nc.vector.quantize_mx(out=z_w[:].bitcast(FP8X4), scales=z_s[:], in_=z16[:].rearrange("p j t -> p (j t)"))
+            return z_w, z_s
+
+        def score(z, j0, n):
+            res = keep.tile([P, PACK, n], F32, name="res%d" % j0)
+            for b0 in range(0, n, BANK_COLS):
+                bank = psum.tile([P, PACK, BANK_COLS], F32, name="bank")
+                for t in range(PACK):
+                    nc.tensor.matmul_mx(
+                        out=bank[:, t, :],
+                        lhsT=cand_w[:, P * t : P * (t + 1)].bitcast(FP8X4),
+                        lhsT_scale=cand_s[:, P * t : P * (t + 1)],
+                        rhs=z[0][:, b0 : b0 + BANK_COLS].bitcast(FP8X4),
+                        rhs_scale=z[1][:, b0 : b0 + BANK_COLS],
+                        start=True,
+                        stop=True,
+                    )
+                nc.scalar.activation(res[:, :, b0 : b0 + BANK_COLS], bank[:], ACT.Copy, scale=0.0625)
+            nc.sync.dma_start(out=out_rows[:, :, j0 : j0 + n], in_=res[:])
+            res16 = keep.tile([P, n, PACK], BF16, name="res16_%d" % j0, align_bytes=64)
+            nc.vector.tensor_copy(
+                res16[:].rearrange("p (c i) t -> p c t i", i=4), res[:].rearrange("p t (c i) -> p c t i", i=4)
+            )
+            nc.vector.quantize_mx(
+                out=out_w[:, j0 : j0 + n].bitcast(FP8X4),
+                scales=out_s[:, j0 : j0 + n],
+                in_=res16[:].rearrange("p j t -> p (j t)"),
+            )
+            nc.sync.dma_start(out=out_words[:, j0 : j0 + n], in_=out_w[:, j0 : j0 + n].bitcast(I32))
+
+        z_prev = None
+        for piece in PIECES:
+            z = make_z(*piece)
+            if z_prev is not None:
+                score(*z_prev)
+            z_prev = (z,) + piece
+        score(*z_prev)
+        for q in range(QUADS):
+            queue = nc.scalar if q % 2 else nc.sync
+            queue.dma_start(
+                out=out_2[0][4 * q : 4 * q + 4, :].bitcast(I32), in_=out_s[32 * q : 32 * q + 4, :].bitcast(I32)
+            )

@@ -21,7 +21,7 @@ PACK = 4
 QUADS = 4
 LANES = 16
 BANK_COLS = 128
-PIECES = ((0, 256), (256, 128), (384, 128))
+HALF = 256
 
 
 def load_scale_rows(queue, plane, rows):
@@ -44,6 +44,7 @@ def tile_picked_gaussprod_none_po_kernel(
     with ExitStack() as ctx:
         lists = ctx.enter_context(tc.tile_pool(name="lists", bufs=1))
         keep = ctx.enter_context(tc.tile_pool(name="keep", bufs=1))
+        ring = ctx.enter_context(tc.tile_pool(name="ring", bufs=2))
         psum = ctx.enter_context(tc.psum_pool(name="psum", bufs=8))
 
         two_l = lists.tile([P, S // LANES], U16, name="two_l")
@@ -57,28 +58,28 @@ def tile_picked_gaussprod_none_po_kernel(
         w1w = keep.tile([P, 2 * H], U8, name="w1w", align_bytes=64)
         w2w = keep.tile([P, 2 * H], U8, name="w2w", align_bytes=64)
         w1s = keep.tile([P, H], U8, name="w1s", align_bytes=64)
-        w2s = keep.tile([P, H], U8, name="w2s", align_bytes=64)
+        w2s = keep.tile([P, H], U8, name="w2s", tag="w2s", align_bytes=64)
         gain = keep.tile([P, PACK], F32, name="gain")
 
-        nc.gpsimd.memset(xs[:].bitcast(I32), 0)
+        nc.vector.memset(xs[:].bitcast(I32), 0)
         nc.vector.memset(w2s[:].bitcast(I32), 0)
         nc.vector.memset(w1s[:].bitcast(I32), 0)
 
         nc.sync.dma_start(two_l[:], two)
         nc.sync.dma_start(offs_l[:], offs)
-        nc.sync.dma_start(out=w2w[:].bitcast(I32), in_=w2_words[0].bitcast(I32))
         load_scale_rows(nc.sync, xs, x_scales[0])
         nc.sync.dma_start(out=xw[:].bitcast(I32), in_=x_words[0].rearrange("p c r -> p (c r)").bitcast(I32))
-        load_scale_rows(nc.scalar, w2s, w2_scales[0])
+        load_scale_rows(nc.sync, w2s, w2_scales[0])
+        nc.sync.dma_start(out=w2w[:].bitcast(I32), in_=w2_words[0].bitcast(I32))
         nc.sync.dma_start(out=w1w[:].bitcast(I32), in_=w1_words[0].bitcast(I32))
+        load_scale_rows(nc.sync, w1s, w1_scales[0])
         nc.sync.dma_start(la_l[:], la)
         nc.sync.dma_start(cand_l[:], cand)
-        load_scale_rows(nc.sync, w1s, w1_scales[0])
+        nc.sync.dma_start(out=gain[:], in_=gs.rearrange("(p t) o -> p (t o)", t=PACK))
         nc.sync.dma_start(lb_l[:], lb)
-        nc.gpsimd.dma_start(out=gain[:], in_=gs.rearrange("(p t) o -> p (t o)", t=PACK))
 
-        def picked(name, offsets):
-            words = keep.tile([P, S], U32, name=name + "_w", align_bytes=64)
+        def picked(name, offsets, words_tag):
+            words = keep.tile([P, S], U32, name=name + "_w", tag=words_tag, align_bytes=64)
             scales = keep.tile([P, S], U8, name=name + "_s", align_bytes=64)
             return words, scales, offsets
 
@@ -95,13 +96,14 @@ def tile_picked_gaussprod_none_po_kernel(
             nc.vector.tensor_copy(dealt(scales_d[:]), undealt(scales[:]))
             return words_d, scales_d
 
-        x_two, x_idx, x_cand = picked("two", two_l), picked("idx", offs_l), picked("cand", cand_l)
+        x_two = picked("pick_a", two_l, "two_w")
         gather_scales(x_two)
-        gather_scales(x_idx)
         w2 = deal_weight("w2", w2w, w2s)
         gather_words(x_two)
-        w1 = deal_weight("w1", w1w, w1s)
+        x_idx = picked("pick_b", offs_l, "w2s")
+        gather_scales(x_idx)
         gather_words(x_idx)
+        w1 = deal_weight("w1", w1w, w1s)
 
         def project(weight, pick, t):
             bank = psum.tile([P, S], F32, name="bank")
@@ -128,20 +130,13 @@ def tile_picked_gaussprod_none_po_kernel(
             nc.vector.scalar_tensor_tensor(u_t[:], y_t[:], gain[:, t : t + 1], pr[t][:], ALU.mult, ALU.mult)
             u.append(u_t)
 
-        gather_scales(x_cand)
-        gather_words(x_cand)
-        cand_w = keep.tile([P, C], U32, name="cand_wd", align_bytes=64)
-        cand_s = keep.tile([P, C], U8, name="cand_sd", align_bytes=64)
-        nc.vector.tensor_copy(dealt(cand_w[:]), undealt(x_cand[0][:]))
-        nc.vector.tensor_copy(dealt(cand_s[:]), undealt(x_cand[1][:]))
-
         out_w = keep.tile([P, S], U32, name="out_w", align_bytes=64)
         out_s = keep.tile([P, S], U8, name="out_s", align_bytes=64)
         out_rows = out_0.rearrange("(p t) j -> p t j", t=PACK)
         out_words = out_1[0].rearrange("p c r -> p (c r)").bitcast(I32)
 
         def fetch_sum(name, tables, j0, n):
-            first = keep.tile([P, PACK, n], F32, name=name + "_a%d" % j0)
+            first = ring.tile([P, PACK, n], F32, name="first")
             total = keep.tile([P, PACK, n], F32, name=name + "_ab%d" % j0)
             cols = slice(j0 // LANES, (j0 + n) // LANES)
             for t in range(PACK):
@@ -149,18 +144,19 @@ def tile_picked_gaussprod_none_po_kernel(
                 nc.vector.tensor_tensor(total[:, t, :], tables[t][:].indirect(lb_l[:, cols]), first[:, t, :], ALU.add)
             return total
 
-        def make_z(j0, n):
-            den = fetch_sum("p", pr, j0, n)
-            num = fetch_sum("u", u, j0, n)
-            root = keep.tile([P, PACK, n], F32, name="root%d" % j0)
-            inv = keep.tile([P, PACK, n], F32, name="inv%d" % j0)
+        def invert(den, j0):
+            root = keep.tile([P, PACK, HALF], F32, name="root%d" % j0)
+            inv = keep.tile([P, PACK, HALF], F32, name="inv%d" % j0)
             nc.scalar.activation(root[:], den[:], ACT.Abs_reciprocal_sqrt, bias=1.0)
             nc.scalar.activation(inv[:], root[:], ACT.Square)
+            return inv
+
+        def make_z(num, inv, j0, n):
             z16 = keep.tile([P, n, PACK], BF16, name="z16_%d" % j0, align_bytes=64)
             nc.vector.tensor_tensor(
                 z16[:].rearrange("p (c i) t -> p c t i", i=4),
                 num[:].rearrange("p t (c i) -> p c t i", i=4),
-                inv[:].rearrange("p t (c i) -> p c t i", i=4),
+                inv[:, :, j0 % HALF : j0 % HALF + n].rearrange("p t (c i) -> p c t i", i=4),
                 ALU.mult,
             )
             z_w = keep.tile([P, n], U32, name="z_w%d" % j0, align_bytes=64)
@@ -168,40 +164,61 @@ def tile_picked_gaussprod_none_po_kernel(
             nc.vector.quantize_mx(out=z_w[:].bitcast(FP8X4), scales=z_s[:], in_=z16[:].rearrange("p j t -> p (j t)"))
             return z_w, z_s
 
-        def score(z, j0, n):
+        def score(z, j0, n, last):
             res = keep.tile([P, PACK, n], F32, name="res%d" % j0)
+            res16 = keep.tile([P, n, PACK], BF16, name="res16_%d" % j0, align_bytes=64)
             for b0 in range(0, n, BANK_COLS):
+                cols = slice(b0, b0 + BANK_COLS)
                 bank = psum.tile([P, PACK, BANK_COLS], F32, name="bank")
                 for t in range(PACK):
                     nc.tensor.matmul_mx(
                         out=bank[:, t, :],
                         lhsT=cand_w[:, P * t : P * (t + 1)].bitcast(FP8X4),
                         lhsT_scale=cand_s[:, P * t : P * (t + 1)],
-                        rhs=z[0][:, b0 : b0 + BANK_COLS].bitcast(FP8X4),
-                        rhs_scale=z[1][:, b0 : b0 + BANK_COLS],
+                        rhs=z[0][:, cols].bitcast(FP8X4),
+                        rhs_scale=z[1][:, cols],
                         start=True,
                         stop=True,
                     )
-                nc.scalar.activation(res[:, :, b0 : b0 + BANK_COLS], bank[:], ACT.Copy, scale=0.0625)
+                woven = bank[:].rearrange("p t j -> p j t")
+                if last:
+                    nc.vector.tensor_scalar(res16[:, cols, :], woven, 0.0625, None, ALU.mult)
+                else:
+                    nc.scalar.activation(res16[:, cols, :], woven, ACT.Copy, scale=0.0625)
+                nc.scalar.activation(res[:, :, cols], bank[:], ACT.Copy, scale=0.0625)
             nc.sync.dma_start(out=out_rows[:, :, j0 : j0 + n], in_=res[:])
-            res16 = keep.tile([P, n, PACK], BF16, name="res16_%d" % j0, align_bytes=64)
-            nc.vector.tensor_copy(
-                res16[:].rearrange("p (c i) t -> p c t i", i=4), res[:].rearrange("p t (c i) -> p c t i", i=4)
-            )
             nc.vector.quantize_mx(
                 out=out_w[:, j0 : j0 + n].bitcast(FP8X4),
                 scales=out_s[:, j0 : j0 + n],
                 in_=res16[:].rearrange("p j t -> p (j t)"),
             )
+
+        def store_words(j0, n):
             nc.sync.dma_start(out=out_words[:, j0 : j0 + n], in_=out_w[:, j0 : j0 + n].bitcast(I32))
 
-        z_prev = None
-        for piece in PIECES:
-            z = make_z(*piece)
-            if z_prev is not None:
-                score(*z_prev)
-            z_prev = (z,) + piece
-        score(*z_prev)
+        x_cand = picked("pick_c", cand_l, "cand_w")
+        gather_scales(x_cand)
+        gather_words(x_cand)
+        cand_w = keep.tile([P, C], U32, name="cand_wd", align_bytes=64)
+        cand_s = keep.tile([P, C], U8, name="cand_sd", align_bytes=64)
+        nc.vector.tensor_copy(dealt(cand_w[:]), undealt(x_cand[0][:]))
+        nc.vector.tensor_copy(dealt(cand_s[:]), undealt(x_cand[1][:]))
+
+        den0 = fetch_sum("p", pr, 0, HALF)
+        num0 = fetch_sum("u", u, 0, HALF)
+        inv0 = invert(den0, 0)
+        den1 = fetch_sum("p", pr, HALF, HALF)
+        z0 = make_z(num0, inv0, 0, HALF)
+        num1 = fetch_sum("u", u, 256, 128)
+        inv1 = invert(den1, HALF)
+        num2 = fetch_sum("u", u, 384, 128)
+        score(z0, 0, HALF, False)
+        store_words(0, HALF)
+        z1 = make_z(num1, inv1, 256, 128)
+        z2 = make_z(num2, inv1, 384, 128)
+        score(z1, 256, 128, False)
+        score(z2, 384, 128, True)
+        store_words(HALF, HALF)
         for q in range(QUADS):
             queue = nc.scalar if q % 2 else nc.sync
             queue.dma_start(

@@ -58,12 +58,12 @@ def tile_picked_gaussprod_none_po_kernel(
         w1w = keep.tile([P, 2 * H], U8, name="w1w", align_bytes=64)
         w2w = keep.tile([P, 2 * H], U8, name="w2w", align_bytes=64)
         w1s = keep.tile([P, H], U8, name="w1s", align_bytes=64)
-        w2s = keep.tile([P, H], U8, name="w2s", tag="w2s", align_bytes=64)
+        w2s = keep.tile([P, H], U8, name="w2s", align_bytes=64)
         gain = keep.tile([P, PACK], F32, name="gain")
 
         nc.vector.memset(xs[:].bitcast(I32), 0)
-        nc.vector.memset(w2s[:].bitcast(I32), 0)
-        nc.vector.memset(w1s[:].bitcast(I32), 0)
+        nc.gpsimd.memset(w2s[:].bitcast(I32), 0)
+        nc.gpsimd.memset(w1s[:].bitcast(I32), 0)
 
         nc.sync.dma_start(two_l[:], two)
         nc.sync.dma_start(offs_l[:], offs)
@@ -78,8 +78,8 @@ def tile_picked_gaussprod_none_po_kernel(
         nc.sync.dma_start(out=gain[:], in_=gs.rearrange("(p t) o -> p (t o)", t=PACK))
         nc.sync.dma_start(lb_l[:], lb)
 
-        def picked(name, offsets, words_tag):
-            words = keep.tile([P, S], U32, name=name + "_w", tag=words_tag, align_bytes=64)
+        def picked(name, offsets):
+            words = keep.tile([P, S], U32, name=name + "_w", align_bytes=64)
             scales = keep.tile([P, S], U8, name=name + "_s", align_bytes=64)
             return words, scales, offsets
 
@@ -93,14 +93,13 @@ def tile_picked_gaussprod_none_po_kernel(
             words_d = keep.tile([P, 2 * H], U8, name=name + "_wd", align_bytes=64)
             scales_d = keep.tile([P, H], U8, name=name + "_sd", align_bytes=64)
             nc.scalar.copy(dealt(words_d[:].bitcast(U16)), undealt(words[:].bitcast(U16)))
-            nc.vector.tensor_copy(dealt(scales_d[:]), undealt(scales[:]))
+            nc.gpsimd.tensor_copy(dealt(scales_d[:]), undealt(scales[:]))
             return words_d, scales_d
 
-        x_two = picked("pick_a", two_l, "two_w")
+        x_two, x_idx = picked("pick_a", two_l), picked("pick_b", offs_l)
         gather_scales(x_two)
         w2 = deal_weight("w2", w2w, w2s)
         gather_words(x_two)
-        x_idx = picked("pick_b", offs_l, "w2s")
         gather_scales(x_idx)
         gather_words(x_idx)
         w1 = deal_weight("w1", w1w, w1s)
@@ -148,7 +147,10 @@ def tile_picked_gaussprod_none_po_kernel(
             root = keep.tile([P, PACK, HALF], F32, name="root%d" % j0)
             inv = keep.tile([P, PACK, HALF], F32, name="inv%d" % j0)
             nc.scalar.activation(root[:], den[:], ACT.Abs_reciprocal_sqrt, bias=1.0)
-            nc.scalar.activation(inv[:], root[:], ACT.Square)
+            if j0 == 0:
+                nc.vector.tensor_tensor(inv[:], root[:], root[:], ALU.mult)
+            else:
+                nc.scalar.activation(inv[:], root[:], ACT.Square)
             return inv
 
         def make_z(num, inv, j0, n):
@@ -164,7 +166,7 @@ def tile_picked_gaussprod_none_po_kernel(
             nc.vector.quantize_mx(out=z_w[:].bitcast(FP8X4), scales=z_s[:], in_=z16[:].rearrange("p j t -> p (j t)"))
             return z_w, z_s
 
-        def score(z, j0, n, last):
+        def score(z, j0, n):
             res = keep.tile([P, PACK, n], F32, name="res%d" % j0)
             res16 = keep.tile([P, n, PACK], BF16, name="res16_%d" % j0, align_bytes=64)
             for b0 in range(0, n, BANK_COLS):
@@ -180,13 +182,11 @@ def tile_picked_gaussprod_none_po_kernel(
                         start=True,
                         stop=True,
                     )
-                woven = bank[:].rearrange("p t j -> p j t")
-                if last:
-                    nc.vector.tensor_scalar(res16[:, cols, :], woven, 0.0625, None, ALU.mult)
-                else:
-                    nc.scalar.activation(res16[:, cols, :], woven, ACT.Copy, scale=0.0625)
                 nc.scalar.activation(res[:, :, cols], bank[:], ACT.Copy, scale=0.0625)
             nc.sync.dma_start(out=out_rows[:, :, j0 : j0 + n], in_=res[:])
+            nc.vector.tensor_copy(
+                res16[:].rearrange("p (c i) t -> p c t i", i=4), res[:].rearrange("p t (c i) -> p c t i", i=4)
+            )
             nc.vector.quantize_mx(
                 out=out_w[:, j0 : j0 + n].bitcast(FP8X4),
                 scales=out_s[:, j0 : j0 + n],
@@ -196,13 +196,10 @@ def tile_picked_gaussprod_none_po_kernel(
         def store_words(j0, n):
             nc.sync.dma_start(out=out_words[:, j0 : j0 + n], in_=out_w[:, j0 : j0 + n].bitcast(I32))
 
-        x_cand = picked("pick_c", cand_l, "cand_w")
-        gather_scales(x_cand)
-        gather_words(x_cand)
         cand_w = keep.tile([P, C], U32, name="cand_wd", align_bytes=64)
         cand_s = keep.tile([P, C], U8, name="cand_sd", align_bytes=64)
-        nc.vector.tensor_copy(dealt(cand_w[:]), undealt(x_cand[0][:]))
-        nc.vector.tensor_copy(dealt(cand_s[:]), undealt(x_cand[1][:]))
+        nc.vector.tensor_copy(cand_s[:].rearrange("p (t m) -> p m t", t=PACK), xs[:].indirect(cand_l[:]))
+        nc.vector.tensor_copy(cand_w[:].rearrange("p (t m) -> p m t", t=PACK), xw[:].indirect(cand_l[:]))
 
         den0 = fetch_sum("p", pr, 0, HALF)
         num0 = fetch_sum("u", u, 0, HALF)
@@ -212,12 +209,12 @@ def tile_picked_gaussprod_none_po_kernel(
         num1 = fetch_sum("u", u, 256, 128)
         inv1 = invert(den1, HALF)
         num2 = fetch_sum("u", u, 384, 128)
-        score(z0, 0, HALF, False)
+        score(z0, 0, HALF)
         store_words(0, HALF)
         z1 = make_z(num1, inv1, 256, 128)
         z2 = make_z(num2, inv1, 384, 128)
-        score(z1, 256, 128, False)
-        score(z2, 384, 128, True)
+        score(z1, 256, 128)
+        score(z2, 384, 128)
         store_words(HALF, HALF)
         for q in range(QUADS):
             queue = nc.scalar if q % 2 else nc.sync

from contextlib import ExitStack

import concourse.mybir as mybir

K, T, S, H, C = 512, 2048, 512, 512, 512
FLOPS = 2 * K * H * S * 2 + 2 * K * C * S

F32 = mybir.dt.float32
BF16 = mybir.dt.bfloat16
I32 = mybir.dt.int32
U32 = mybir.dt.uint32
U16 = mybir.dt.uint16
U8 = mybir.dt.uint8
FP8X4 = mybir.dt.float8_e4m3fn_x4
FP4X4 = mybir.dt.float4_e2m1fn_x4
ACT = mybir.ActivationFunctionType
ALU = mybir.AluOpType

P = 128
PACK = 4
QUADS = 4
LANES = 16
BANK_COLS = 128
HALF = 256


def load_scale_rows(queue, plane, rows):
    for q in range(QUADS):
        queue.dma_start(out=plane[32 * q : 32 * q + 4, :].bitcast(I32), in_=rows[4 * q : 4 * q + 4, :].bitcast(I32))


def dealt(ap):
    return ap.rearrange("p (t m) -> p t m", t=PACK)


def undealt(ap):
    return ap.rearrange("p (m t) -> p t m", t=PACK)


def tile_picked_gaussprod_none_po_kernel(
    tc, x_words, x_scales, w1_words, w1_scales, w2_words, w2_scales, gs, offs, two, la, lb, cand, out_0, out_1, out_2
):
    nc = tc.nc
    with ExitStack() as ctx:
        lists = ctx.enter_context(tc.tile_pool(name="lists", bufs=1))
        keep = ctx.enter_context(tc.tile_pool(name="keep", bufs=1))
        ring = ctx.enter_context(tc.tile_pool(name="ring", bufs=2))
        psum = ctx.enter_context(tc.psum_pool(name="psum", bufs=8))

        two_l = lists.tile([P, S // LANES], U16, name="two_l")
        offs_l = lists.tile([P, S // LANES], U16, name="offs_l")
        cand_l = lists.tile([P, C // LANES], U16, name="cand_l")
        la_l = lists.tile([P, S // LANES], U16, name="la_l")
        lb_l = lists.tile([P, S // LANES], U16, name="lb_l")

        xw = keep.tile([P, T], U32, name="xw", align_bytes=64)
        xs = keep.tile([P, T], U8, name="xs", align_bytes=64)
        w1w = keep.tile([P, 2 * H], U8, name="w1w", align_bytes=64)
        w2w = keep.tile([P, 2 * H], U8, name="w2w", align_bytes=64)
        w1s = keep.tile([P, H], U8, name="w1s", align_bytes=64)
        w2s = keep.tile([P, H], U8, name="w2s", align_bytes=64)
        gain = keep.tile([P, PACK], F32, name="gain")

        nc.vector.memset(xs[:].bitcast(I32), 0)
        nc.gpsimd.memset(w2s[:].bitcast(I32), 0)
        nc.gpsimd.memset(w1s[:].bitcast(I32), 0)

        nc.sync.dma_start(two_l[:], two)
        nc.sync.dma_start(offs_l[:], offs)
        load_scale_rows(nc.sync, xs, x_scales[0])
        nc.sync.dma_start(out=xw[:].bitcast(I32), in_=x_words[0].rearrange("p c r -> p (c r)").bitcast(I32))
        load_scale_rows(nc.sync, w2s, w2_scales[0])
        nc.sync.dma_start(out=w2w[:].bitcast(I32), in_=w2_words[0].bitcast(I32))
        nc.sync.dma_start(out=w1w[:].bitcast(I32), in_=w1_words[0].bitcast(I32))
        load_scale_rows(nc.sync, w1s, w1_scales[0])
        nc.sync.dma_start(la_l[:], la)
        nc.sync.dma_start(cand_l[:], cand)
        nc.sync.dma_start(out=gain[:], in_=gs.rearrange("(p t) o -> p (t o)", t=PACK))
        nc.sync.dma_start(lb_l[:], lb)

        def picked(name, offsets):
            words = keep.tile([P, S], U32, name=name + "_w", align_bytes=64)
            scales = keep.tile([P, S], U8, name=name + "_s", align_bytes=64)
            return words, scales, offsets

        def gather_scales(pick):
            nc.vector.tensor_copy(pick[1][:], xs[:].indirect(pick[2][:]))

        def gather_words(pick):
            nc.vector.tensor_copy(pick[0][:], xw[:].indirect(pick[2][:]))

        def deal_weight(name, words, scales):
            words_d = keep.tile([P, 2 * H], U8, name=name + "_wd", align_bytes=64)
            scales_d = keep.tile([P, H], U8, name=name + "_sd", align_bytes=64)
            nc.scalar.copy(dealt(words_d[:].bitcast(U16)), undealt(words[:].bitcast(U16)))
            nc.gpsimd.tensor_copy(dealt(scales_d[:]), undealt(scales[:]))
            return words_d, scales_d

        x_two, x_idx = picked("pick_a", two_l), picked("pick_b", offs_l)
        gather_scales(x_two)
        w2 = deal_weight("w2", w2w, w2s)
        gather_words(x_two)
        gather_scales(x_idx)
        gather_words(x_idx)
        w1 = deal_weight("w1", w1w, w1s)

        def project(weight, pick, t):
            bank = psum.tile([P, S], F32, name="bank")
            nc.tensor.matmul_mx(
                out=bank[:],
                lhsT=weight[0][:, 2 * P * t : 2 * P * (t + 1)].bitcast(FP4X4),
                lhsT_scale=weight[1][:, P * t : P * (t + 1)],
                rhs=pick[0][:].bitcast(FP8X4),
                rhs_scale=pick[1][:],
                start=True,
                stop=True,
            )
            return bank

        pr, u = [], []
        for t in range(PACK):
            c_t = project(w2, x_two, t)
            pr_t = keep.tile([P, S], F32, name="pr%d" % t)
            nc.scalar.activation(pr_t[:], c_t[:], ACT.Exp, scale=0.5)
            pr.append(pr_t)
        for t in range(PACK):
            y_t = project(w1, x_idx, t)
            u_t = keep.tile([P, S], F32, name="u%d" % t)
            nc.vector.scalar_tensor_tensor(u_t[:], y_t[:], gain[:, t : t + 1], pr[t][:], ALU.mult, ALU.mult)
            u.append(u_t)

        out_w = keep.tile([P, S], U32, name="out_w", align_bytes=64)
        out_s = keep.tile([P, S], U8, name="out_s", align_bytes=64)
        out_rows = out_0.rearrange("(p t) j -> p t j", t=PACK)
        out_words = out_1[0].rearrange("p c r -> p (c r)").bitcast(I32)

        def fetch_sum(name, tables, j0, n):
            first = ring.tile([P, PACK, n], F32, name="first")
            total = keep.tile([P, PACK, n], F32, name=name + "_ab%d" % j0)
            cols = slice(j0 // LANES, (j0 + n) // LANES)
            for t in range(PACK):
                nc.scalar.activation(first[:, t, :], tables[t][:].indirect(la_l[:, cols]), ACT.Copy)
                nc.vector.tensor_tensor(total[:, t, :], tables[t][:].indirect(lb_l[:, cols]), first[:, t, :], ALU.add)
            return total

        def invert(den, j0):
            root = keep.tile([P, PACK, HALF], F32, name="root%d" % j0)
            inv = keep.tile([P, PACK, HALF], F32, name="inv%d" % j0)
            nc.scalar.activation(root[:], den[:], ACT.Abs_reciprocal_sqrt, bias=1.0)
            if j0 == 0:
                nc.vector.tensor_tensor(inv[:], root[:], root[:], ALU.mult)
            else:
                nc.scalar.activation(inv[:], root[:], ACT.Square)
            return inv

        def make_z(num, inv, j0, n):
            z16 = keep.tile([P, n, PACK], BF16, name="z16_%d" % j0, align_bytes=64)
            nc.vector.tensor_tensor(
                z16[:].rearrange("p (c i) t -> p c t i", i=4),
                num[:].rearrange("p t (c i) -> p c t i", i=4),
                inv[:, :, j0 % HALF : j0 % HALF + n].rearrange("p t (c i) -> p c t i", i=4),
                ALU.mult,
            )
            z_w = keep.tile([P, n], U32, name="z_w%d" % j0, align_bytes=64)
            z_s = keep.tile([P, n], U8, name="z_s%d" % j0, align_bytes=64)
            nc.vector.quantize_mx(out=z_w[:].bitcast(FP8X4), scales=z_s[:], in_=z16[:].rearrange("p j t -> p (j t)"))
            return z_w, z_s

        def score(z, j0, n):
            res = keep.tile([P, PACK, n], F32, name="res%d" % j0)
            res16 = keep.tile([P, n, PACK], BF16, name="res16_%d" % j0, align_bytes=64)
            for b0 in range(0, n, BANK_COLS):
                cols = slice(b0, b0 + BANK_COLS)
                bank = psum.tile([P, PACK, BANK_COLS], F32, name="bank")
                for t in range(PACK):
                    nc.tensor.matmul_mx(
                        out=bank[:, t, :],
                        lhsT=cand_w[:, P * t : P * (t + 1)].bitcast(FP8X4),
                        lhsT_scale=cand_s[:, P * t : P * (t + 1)],
                        rhs=z[0][:, cols].bitcast(FP8X4),
                        rhs_scale=z[1][:, cols],
                        start=True,
                        stop=True,
                    )
                nc.scalar.activation(res[:, :, cols], bank[:], ACT.Copy, scale=0.0625)
            nc.sync.dma_start(out=out_rows[:, :, j0 : j0 + n], in_=res[:])
            nc.vector.tensor_copy(
                res16[:].rearrange("p (c i) t -> p c t i", i=4), res[:].rearrange("p t (c i) -> p c t i", i=4)
            )
            nc.vector.quantize_mx(
                out=out_w[:, j0 : j0 + n].bitcast(FP8X4),
                scales=out_s[:, j0 : j0 + n],
                in_=res16[:].rearrange("p j t -> p (j t)"),
            )

        def store_words(j0, n):
            nc.sync.dma_start(out=out_words[:, j0 : j0 + n], in_=out_w[:, j0 : j0 + n].bitcast(I32))

        cand_w = keep.tile([P, C], U32, name="cand_wd", align_bytes=64)
        cand_s = keep.tile([P, C], U8, name="cand_sd", align_bytes=64)
        nc.vector.tensor_copy(cand_s[:].rearrange("p (t m) -> p m t", t=PACK), xs[:].indirect(cand_l[:]))
        nc.vector.tensor_copy(cand_w[:].rearrange("p (t m) -> p m t", t=PACK), xw[:].indirect(cand_l[:]))

        den0 = fetch_sum("p", pr, 0, HALF)
        num0 = fetch_sum("u", u, 0, HALF)
        inv0 = invert(den0, 0)
        den1 = fetch_sum("p", pr, HALF, HALF)
        z0 = make_z(num0, inv0, 0, HALF)
        num1 = fetch_sum("u", u, 256, 128)
        inv1 = invert(den1, HALF)
        num2 = fetch_sum("u", u, 384, 128)
        score(z0, 0, HALF)
        store_words(0, HALF)
        z1 = make_z(num1, inv1, 256, 128)
        z2 = make_z(num2, inv1, 384, 128)
        score(z1, 256, 128)
        score(z2, 384, 128)
        store_words(HALF, HALF)
        for q in range(QUADS):
            queue = nc.scalar if q % 2 else nc.sync
            queue.dma_start(
                out=out_2[0][4 * q : 4 * q + 4, :].bitcast(I32), in_=out_s[32 * q : 32 * q + 4, :].bitcast(I32)
            )
